import numpy as np
import ml_dtypes


def mxq(x, axis, fmt="e4m3"):
    dtype, down = {"e4m3": (ml_dtypes.float8_e4m3fn, 7), "e5m2": (ml_dtypes.float8_e5m2, 14)}[fmt]
    v = np.moveaxis(np.asarray(x, np.float32).astype(ml_dtypes.bfloat16).astype(np.float64), axis, -1)
    blocks = v.reshape(v.shape[:-1] + (-1, 32))
    amax = np.abs(blocks).max(-1, keepdims=True)
    byte = np.maximum(np.where(amax > 0, np.frexp(amax)[1] - 1 + 127, 0) - down, 1)
    scale = np.exp2(byte - 127.0)
    codes = (blocks / scale).astype(np.float32).astype(dtype).astype(np.float64)
    return np.moveaxis((codes * scale).reshape(v.shape), -1, axis)


WIDE = False


def mx_kscale(k):
    if not WIDE:
        return np.ones(k)
    levels = np.array([10, -10, 5, -5, 0])
    if k % 512:
        return np.exp2(np.random.permutation(np.resize(levels, k // 32))).repeat(32)
    a = np.empty((k // 512, 16))
    for p in range(k // 512):
        a[p, :8] = np.random.permutation(np.resize(levels, 8))
        for g in range(8):
            far = levels[np.abs(levels - a[p, g]) >= 10]
            a[p, g + 8] = far[np.random.randint(len(far))]
    return np.exp2(a.ravel()).repeat(32)


def f64(x):
    return np.asarray(x).astype(np.float64)


def striped(idx):
    return np.tile(np.asarray(idx).reshape(-1, 16).T, (8, 1)).astype(np.uint16)


def unstriped(offs):
    return offs[:16].T.reshape(-1).astype(np.int64)


def striped8(idx):
    return np.asarray(idx).reshape(8, -1, 16).transpose(0, 2, 1).reshape(128, -1).astype(np.uint16)


def unstriped8(offs):
    return offs.reshape(8, 16, -1).transpose(0, 2, 1).reshape(8, -1).astype(np.int64)


def pick8(x, idx, run):
    r = np.arange(len(x))
    return x[r[:, None], idx[r % (8 * run) // run]]


E2M1 = np.array([0.0, 0.5, 1.0, 1.5, 2.0, 3.0, 4.0, 6.0, -0.0, -0.5, -1.0, -1.5, -2.0, -3.0, -4.0, -6.0])


def pack_weight(w, fmt):
    k, n = w.shape
    w = f64(np.asarray(w, np.float32).astype(ml_dtypes.bfloat16)).reshape(k // 32, 32, n)
    amax = np.abs(w).max(1)
    if fmt == "e4m3":
        byte = np.frexp(amax)[1] - 1 + 127 - 7
    else:
        mant, ex = np.frexp(amax / 6.0)
        byte = np.where(mant > 0.5, ex, ex - 1) + 127
    byte = np.clip(np.where(amax > 0, byte, 1), 1, 254)
    scaled = (w * np.exp2(127.0 - byte)[:, None, :]).reshape(k, n).astype(np.float32)
    by_word = np.ascontiguousarray(scaled.reshape(k // 512, 128, 4, n).transpose(0, 1, 3, 2))
    if fmt == "e4m3":
        words = by_word.astype(ml_dtypes.float8_e4m3fn).view(np.uint8)
    else:
        c = by_word.astype(ml_dtypes.float4_e2m1fn).view(np.uint8) & 0xF
        words = (c[..., 0::2] | (c[..., 1::2] << 4)).reshape(k // 512, 128, 2 * n)
    return np.ascontiguousarray(words), np.ascontiguousarray(byte.astype(np.uint8).reshape(k // 512, 16, n))


def unpack_weight(words, scales, fmt):
    g, _, n = scales.shape
    words = np.ascontiguousarray(words).reshape(g, 128, n, -1)
    if fmt == "e4m3":
        vals = words.view(ml_dtypes.float8_e4m3fn).astype(np.float64)
    else:
        nib = np.empty((g, 128, n, 4), np.uint8)
        nib[..., 0::2] = words & 0xF
        nib[..., 1::2] = words >> 4
        vals = E2M1[nib]
    vals = vals * np.repeat(np.exp2(scales.astype(np.float64) - 127.0), 8, axis=1)[..., None]
    return vals.transpose(0, 1, 3, 2).reshape(g * 512, n)


K, J, R, T, U, C, O, S, N, Z = 512, 256, 512, 1024, 1024, 512, 128, 256, 256, 1024


def setup_inputs():
    n = np.random.standard_normal
    idx = np.stack([np.random.permutation(T)[:J] for _ in range(8)])
    idx2 = np.stack([np.random.permutation(U)[:J] for _ in range(8)])
    idx3 = np.stack([np.random.permutation(C)[:J] for _ in range(8)])
    idx4 = np.stack([np.random.permutation(C)[:S] for _ in range(8)])
    idx5 = np.random.permutation(C)[:S]
    idx6 = np.stack([np.random.permutation(S)[:O] for _ in range(8)])
    idx7 = np.random.permutation(Z)[:N]
    fk = mx_kscale(K)
    fr = mx_kscale(R)
    wp = pack_weight(n((K, R)) * 1 / np.sqrt(K) / fk[:, None] * fr, "e2m1")
    vsp = pack_weight(n((R, Z)) * 1 / np.sqrt(R) / fr[:, None], "e4m3")
    return {
        "ta": (np.random.randint(-7, 8, (K, T)).astype(np.float64)).astype(np.float32),
        "tb": (np.random.randint(-7, 8, (K, U)).astype(np.float64)).astype(np.float32),
        "ga": ((np.random.randint(8, 25, (K, 1)) / 64.0) * fk[:, None]).astype(np.float32),
        "gb": ((np.random.randint(8, 25, (K, 1)) / 64.0) * fk[:, None]).astype(np.float32),
        "w_words": wp[0],
        "w_scales": wp[1],
        "sa": (np.random.uniform(0.5, 1.6, (R, 1))).astype(np.float32),
        "sb": (np.random.uniform(0.5, 1.6, (R, 1))).astype(np.float32),
        "sd": (np.random.uniform(0.5, 1.6, (R, 1))).astype(np.float32),
        "vs_words": vsp[0],
        "vs_scales": vsp[1],
        "offs": striped8(idx),
        "offs2": striped8(idx2),
        "offs3": striped8(idx3),
        "offs4": striped8(idx4),
        "offs5": striped(idx5),
        "offs6": striped8(idx6),
        "offs7": striped(idx7),
    }


def reference(ta, tb, ga, gb, w_words, w_scales, sa, sb, sd, vs_words, vs_scales, offs, offs2, offs3, offs4, offs5, offs6, offs7):
    idx = unstriped8(offs)
    idx2 = unstriped8(offs2)
    idx3 = unstriped8(offs3)
    idx4 = unstriped8(offs4)
    idx5 = unstriped(offs5)
    idx6 = unstriped8(offs6)
    idx7 = unstriped(offs7)
    wu = unpack_weight(w_words, w_scales, "e2m1")
    vsu = unpack_weight(vs_words, vs_scales, "e4m3")
    xc = np.maximum(pick8(f64(ta), idx, 64) * f64(ga), pick8(f64(tb), idx2, 64) * f64(gb))
    xcq = mxq(xc, 0, "e4m3")
    a = wu.T @ xcq
    pw = np.zeros((R, C))
    pw[np.arange(R)[:, None], idx3[np.arange(R) % 512 // 64]] = a
    pg = np.maximum(pick8(pw, idx4, 64) * f64(sa), pw[:, idx5] * f64(sb))
    hid = pick8(pg, idx6, 64) * f64(sd)
    vsidx7g = vsu[:, idx7]
    hidq = mxq(hid, 0, "e4m3")
    y = vsidx7g.T @ hidq
    return y

@@ -1,0 +1,188 @@
+from contextlib import ExitStack
+
+import concourse.mybir as mybir
+
+K, J, R, T, U, C, O, S, N, Z = 512, 256, 512, 1024, 1024, 512, 128, 256, 256, 1024
+FLOPS = 2 * K * R * J + 2 * R * N * O
+
+F32 = mybir.dt.float32
+BF16 = mybir.dt.bfloat16
+I32 = mybir.dt.int32
+U32 = mybir.dt.uint32
+U16 = mybir.dt.uint16
+U8 = mybir.dt.uint8
+FP8X4 = mybir.dt.float8_e4m3fn_x4
+FP4X4 = mybir.dt.float4_e2m1fn_x4
+COPY = mybir.ActivationFunctionType.Copy
+MAX = mybir.AluOpType.max
+
+P = 128
+PACK = 4
+HALF = J // 2
+
+
+def interleave(nc, dst, src):
+    nc.vector.tensor_copy(
+        out=dst.rearrange("p (c i t) -> p c t i", i=4, t=PACK),
+        in_=src.rearrange("p t (c i) -> p c t i", i=4),
+    )
+
+
+def tile_picked_largercode_plain_one_ladder_store_plain_kernel(
+    tc, ta, tb, ga, gb, w_words, w_scales, sa, sb, sd, vs_words, vs_scales,
+    offs, offs2, offs3, offs4, offs5, offs6, offs7, out,
+):
+    nc = tc.nc
+    with ExitStack() as ctx:
+        lists = ctx.enter_context(tc.tile_pool(name="lists", bufs=1))
+        pool = ctx.enter_context(tc.tile_pool(name="pool", bufs=1))
+        psum = ctx.enter_context(tc.psum_pool(name="psum", bufs=1))
+
+        def load_list(src, name):
+            tile = lists.tile(list(src.shape), U16, name=name)
+            nc.sync.dma_start(tile[:], src)
+            return tile
+
+        def load_factor(src, name):
+            tile = pool.tile([P, PACK], F32, name=name)
+            nc.sync.dma_start(tile[:], src.rearrange("(p t) o -> p (t o)", t=PACK))
+            return tile
+
+        def load_rows(src, t, name):
+            tile = pool.tile([P, src.shape[1]], F32, name=name)
+            nc.sync.dma_start(tile[:], src.rearrange("(p t) c -> t p c", t=PACK)[t])
+            return tile
+
+        w_plane = pool.tile([P, R], U8, name="w_plane", align_bytes=64)
+        nc.vector.memset(w_plane[:].bitcast(I32), 0)
+        vs_plane = pool.tile([P, Z], U8, name="vs_plane", align_bytes=64)
+        nc.vector.memset(vs_plane[:].bitcast(I32), 0)
+        pw = [pool.tile([P, C], F32, name=f"pw{t}") for t in range(PACK)]
+        for t in range(PACK):
+            nc.vector.memset(pw[t][:], 0.0)
+
+        ta_sb, tb_sb = {}, {}
+        ta_sb[0] = load_rows(ta, 0, "ta0")
+        l1 = load_list(offs, "l1")
+        ga_sb = load_factor(ga, "ga_sb")
+        tb_sb[0] = load_rows(tb, 0, "tb0")
+        l2 = load_list(offs2, "l2")
+        gb_sb = load_factor(gb, "gb_sb")
+        ta_sb[1] = load_rows(ta, 1, "ta1")
+        tb_sb[1] = load_rows(tb, 1, "tb1")
+        ta_sb[2] = load_rows(ta, 2, "ta2")
+        w_raw = pool.tile([P, 2 * R], U8, name="w_raw", align_bytes=64)
+        nc.sync.dma_start(w_raw[:].bitcast(I32), w_words[0].bitcast(I32))
+        w_stage = pool.tile([4, 4, R // 4], I32, name="w_stage")
+        nc.sync.dma_start(w_stage[:], w_scales[0].bitcast(I32).rearrange("(q i) n -> i q n", i=4))
+        tb_sb[2] = load_rows(tb, 2, "tb2")
+        ta_sb[3] = load_rows(ta, 3, "ta3")
+        tb_sb[3] = load_rows(tb, 3, "tb3")
+        l3 = load_list(offs3, "l3")
+        l4 = load_list(offs4, "l4")
+        sa_sb = load_factor(sa, "sa_sb")
+        l5 = load_list(offs5, "l5")
+        sb_sb = load_factor(sb, "sb_sb")
+        l6 = load_list(offs6, "l6")
+        sd_sb = load_factor(sd, "sd_sb")
+        l7 = load_list(offs7, "l7")
+        vs_raw = pool.tile([P, Z], I32, name="vs_raw")
+        nc.sync.dma_start(vs_raw[:], vs_words[0].rearrange("p n t -> p (n t)").bitcast(I32))
+        for q in range(4):
+            nc.sync.dma_start(
+                vs_plane[32 * q : 32 * q + 4, :].bitcast(I32),
+                vs_scales[0, 4 * q : 4 * q + 4, :].bitcast(I32),
+            )
+
+        w_codes = pool.tile([P, 2 * R], U8, name="w_codes", align_bytes=64)
+        nc.vector.tensor_copy(
+            out=w_codes[:].rearrange("p (t m b) -> p t m b", t=PACK, b=2),
+            in_=w_raw[:].rearrange("p (m t b) -> p t m b", t=PACK, b=2),
+        )
+        for q in range(4):
+            nc.vector.tensor_copy(out=w_plane[32 * q : 32 * q + 4, :].bitcast(I32), in_=w_stage[:, q, :])
+        w_sc = pool.tile([P, R], U8, name="w_sc", align_bytes=64)
+        nc.vector.tensor_copy(
+            out=w_sc[:].rearrange("p (t m) -> p t m", t=PACK),
+            in_=w_plane[:].rearrange("p (m t) -> p t m", t=PACK),
+        )
+
+        xc = [pool.tile([P, PACK, HALF], BF16, name=f"xc{h}") for h in range(2)]
+        for t in range(PACK):
+            pa = pool.tile([P, J], F32, name=f"pa{t}")
+            pb = pool.tile([P, J], F32, name=f"pb{t}")
+            nc.scalar.activation(out=pa[:], in_=ta_sb[t][:].indirect(l1[:]), func=COPY, scale=ga_sb[:, t : t + 1])
+            nc.scalar.activation(out=pb[:], in_=tb_sb[t][:].indirect(l2[:]), func=COPY, scale=gb_sb[:, t : t + 1])
+            for h in range(2):
+                cols = slice(h * HALF, (h + 1) * HALF)
+                nc.vector.tensor_tensor(out=xc[h][:, t, :], in0=pa[:, cols], in1=pb[:, cols], op=MAX)
+        xc_il = [pool.tile([P, PACK * HALF], BF16, name=f"xc_il{h}", align_bytes=64) for h in range(2)]
+        for h in range(2):
+            interleave(nc, xc_il[h][:], xc[h][:])
+        x_codes = pool.tile([P, J], U32, name="x_codes", align_bytes=64)
+        x_sc = pool.tile([P, J], U8, name="x_sc", align_bytes=64)
+        for h in range(2):
+            cols = slice(h * HALF, (h + 1) * HALF)
+            nc.vector.quantize_mx(out=x_codes[:, cols].bitcast(FP8X4), scales=x_sc[:, cols], in_=xc_il[h][:])
+
+        pieces = [(0, 0, HALF), (0, HALF, J)] + [(t, 0, J) for t in range(1, PACK)]
+        staged = []
+        for t, j0, j1 in pieces:
+            acc = psum.tile([P, j1 - j0], F32, name=f"a_ps{t}_{j0}")
+            nc.tensor.matmul_mx(
+                out=acc[:],
+                lhsT=w_codes[:, 2 * P * t : 2 * P * (t + 1)].bitcast(FP4X4),
+                lhsT_scale=w_sc[:, P * t : P * (t + 1)],
+                rhs=x_codes[:, j0:j1].bitcast(FP8X4),
+                rhs_scale=x_sc[:, j0:j1],
+                start=True,
+                stop=True,
+            )
+            a_sb = pool.tile([P, j1 - j0], F32, name=f"a_sb{t}_{j0}")
+            nc.scalar.copy(out=a_sb[:], in_=acc[:])
+            staged.append(a_sb)
+        for (t, j0, j1), a_sb in zip(pieces, staged):
+            nc.vector.tensor_copy(out=pw[t][:].indirect(l3[:, j0 // 16 : j1 // 16]), in_=a_sb[:])
+
+        own, shared = [], []
+        for t in range(PACK):
+            own.append(pool.tile([P, S], F32, name=f"own{t}", tag=f"own{t}", align_bytes=64))
+            shared.append(pool.tile([P, S], F32, name=f"shared{t}"))
+            nc.scalar.activation(out=own[t][:], in_=pw[t][:].indirect(l4[:]), func=COPY, scale=sa_sb[:, t : t + 1])
+            nc.scalar.activation(out=shared[t][:], in_=pw[t][:].indirect(l5[:]), func=COPY, scale=sb_sb[:, t : t + 1])
+        pg = [pool.tile([P, S], F32, name=f"pg{t}") for t in range(PACK)]
+        for t in range(PACK):
+            nc.vector.tensor_tensor(out=pg[t][:], in0=own[t][:], in1=shared[t][:], op=MAX)
+        hid = pool.tile([P, PACK, O], BF16, name="hid")
+        for t in range(PACK):
+            nc.scalar.activation(out=hid[:, t, :], in_=pg[t][:].indirect(l6[:]), func=COPY, scale=sd_sb[:, t : t + 1])
+
+        vs_sc = pool.tile([P, N], U8, name="vs_sc", tag="own2", align_bytes=64)
+        nc.vector.tensor_copy(out=vs_sc[:], in_=vs_plane[:].indirect(l7[:]))
+        vs_codes = pool.tile([P, N], U32, name="vs_codes", tag="own3", align_bytes=64)
+        nc.vector.tensor_copy(out=vs_codes[:], in_=vs_raw[:].bitcast(U32).indirect(l7[:]))
+
+        hid_il = pool.tile([P, PACK * O], BF16, name="hid_il", align_bytes=64)
+        interleave(nc, hid_il[:], hid[:])
+        h_codes = pool.tile([P, O], U32, name="h_codes", align_bytes=64)
+        h_sc = pool.tile([P, O], U8, name="h_sc", align_bytes=64)
+        nc.vector.quantize_mx(out=h_codes[:].bitcast(FP8X4), scales=h_sc[:], in_=hid_il[:])
+        for u in range(2):
+            rows = slice(u * P, (u + 1) * P)
+            y_ps = psum.tile([P, O], F32, name=f"y_ps{u}")
+            nc.tensor.matmul_mx(
+                out=y_ps[:],
+                lhsT=vs_codes[:, rows].bitcast(FP8X4),
+                lhsT_scale=vs_sc[:, rows],
+                rhs=h_codes[:].bitcast(FP8X4),
+                rhs_scale=h_sc[:],
+                start=True,
+                stop=True,
+            )
+            y_sb = pool.tile([P, O], F32, name=f"y_sb{u}")
+            if u == 0:
+                nc.scalar.copy(out=y_sb[:], in_=y_ps[:])
+                nc.scalar.dma_start(out[rows, :], y_sb[:])
+            else:
+                nc.vector.tensor_copy(out=y_sb[:], in_=y_ps[:])
+                nc.sync.dma_start(out[rows, :], y_sb[:])

@@ -21,13 +21,6 @@ PACK = 4
 HALF = J // 2
 
 
-def interleave(nc, dst, src):
-    nc.vector.tensor_copy(
-        out=dst.rearrange("p (c i t) -> p c t i", i=4, t=PACK),
-        in_=src.rearrange("p t (c i) -> p c t i", i=4),
-    )
-
-
 def tile_picked_largercode_plain_one_ladder_store_plain_kernel(
     tc, ta, tb, ga, gb, w_words, w_scales, sa, sb, sd, vs_words, vs_scales,
     offs, offs2, offs3, offs4, offs5, offs6, offs7, out,
@@ -44,7 +37,7 @@ def tile_picked_largercode_plain_one_ladder_store_plain_kernel(
             return tile
 
         def load_factor(src, name):
-            tile = pool.tile([P, PACK], F32, name=name)
+            tile = pool.tile([P, PACK], F32, name=name, tag=name)
             nc.sync.dma_start(tile[:], src.rearrange("(p t) o -> p (t o)", t=PACK))
             return tile
 
@@ -69,12 +62,12 @@ def tile_picked_largercode_plain_one_ladder_store_plain_kernel(
         l2 = load_list(offs2, "l2")
         gb_sb = load_factor(gb, "gb_sb")
         ta_sb[1] = load_rows(ta, 1, "ta1")
-        tb_sb[1] = load_rows(tb, 1, "tb1")
-        ta_sb[2] = load_rows(ta, 2, "ta2")
         w_raw = pool.tile([P, 2 * R], U8, name="w_raw", align_bytes=64)
         nc.sync.dma_start(w_raw[:].bitcast(I32), w_words[0].bitcast(I32))
+        tb_sb[1] = load_rows(tb, 1, "tb1")
         w_stage = pool.tile([4, 4, R // 4], I32, name="w_stage")
         nc.sync.dma_start(w_stage[:], w_scales[0].bitcast(I32).rearrange("(q i) n -> i q n", i=4))
+        ta_sb[2] = load_rows(ta, 2, "ta2")
         tb_sb[2] = load_rows(tb, 2, "tb2")
         ta_sb[3] = load_rows(ta, 3, "ta3")
         tb_sb[3] = load_rows(tb, 3, "tb3")
@@ -83,11 +76,11 @@ def tile_picked_largercode_plain_one_ladder_store_plain_kernel(
         sa_sb = load_factor(sa, "sa_sb")
         l5 = load_list(offs5, "l5")
         sb_sb = load_factor(sb, "sb_sb")
-        l6 = load_list(offs6, "l6")
-        sd_sb = load_factor(sd, "sd_sb")
         l7 = load_list(offs7, "l7")
         vs_raw = pool.tile([P, Z], I32, name="vs_raw")
         nc.sync.dma_start(vs_raw[:], vs_words[0].rearrange("p n t -> p (n t)").bitcast(I32))
+        l6 = load_list(offs6, "l6")
+        sd_sb = load_factor(sd, "sd_sb")
         for q in range(4):
             nc.sync.dma_start(
                 vs_plane[32 * q : 32 * q + 4, :].bitcast(I32),
@@ -107,7 +100,7 @@ def tile_picked_largercode_plain_one_ladder_store_plain_kernel(
             in_=w_plane[:].rearrange("p (m t) -> p t m", t=PACK),
         )
 
-        xc = [pool.tile([P, PACK, HALF], BF16, name=f"xc{h}") for h in range(2)]
+        xc_il = [pool.tile([P, HALF, PACK], BF16, name=f"xc_il{h}", tag=f"xc_il{h}", align_bytes=64) for h in range(2)]
         for t in range(PACK):
             pa = pool.tile([P, J], F32, name=f"pa{t}")
             pb = pool.tile([P, J], F32, name=f"pb{t}")
@@ -115,18 +108,17 @@ def tile_picked_largercode_plain_one_ladder_store_plain_kernel(
             nc.scalar.activation(out=pb[:], in_=tb_sb[t][:].indirect(l2[:]), func=COPY, scale=gb_sb[:, t : t + 1])
             for h in range(2):
                 cols = slice(h * HALF, (h + 1) * HALF)
-                nc.vector.tensor_tensor(out=xc[h][:, t, :], in0=pa[:, cols], in1=pb[:, cols], op=MAX)
-        xc_il = [pool.tile([P, PACK * HALF], BF16, name=f"xc_il{h}", align_bytes=64) for h in range(2)]
-        for h in range(2):
-            interleave(nc, xc_il[h][:], xc[h][:])
+                nc.vector.tensor_tensor(out=xc_il[h][:, :, t], in0=pa[:, cols], in1=pb[:, cols], op=MAX)
         x_codes = pool.tile([P, J], U32, name="x_codes", align_bytes=64)
         x_sc = pool.tile([P, J], U8, name="x_sc", align_bytes=64)
         for h in range(2):
             cols = slice(h * HALF, (h + 1) * HALF)
-            nc.vector.quantize_mx(out=x_codes[:, cols].bitcast(FP8X4), scales=x_sc[:, cols], in_=xc_il[h][:])
+            nc.vector.quantize_mx(out=x_codes[:, cols].bitcast(FP8X4), scales=x_sc[:, cols], in_=xc_il[h][:].rearrange("p c t -> p (c t)"))
 
-        pieces = [(0, 0, HALF), (0, HALF, J)] + [(t, 0, J) for t in range(1, PACK)]
-        staged = []
+        vs_codes = pool.tile([P, N], U32, name="vs_codes", tag="xc_il1", align_bytes=64)
+        nc.vector.tensor_copy(out=vs_codes[:], in_=vs_raw[:].bitcast(U32).indirect(l7[:]))
+        pieces = [(0, 0, HALF), (1, 0, HALF), (0, HALF, J), (1, HALF, J), (2, 0, J), (3, 0, J)]
+        accs = []
         for t, j0, j1 in pieces:
             acc = psum.tile([P, j1 - j0], F32, name=f"a_ps{t}_{j0}")
             nc.tensor.matmul_mx(
@@ -138,10 +130,10 @@ def tile_picked_largercode_plain_one_ladder_store_plain_kernel(
                 start=True,
                 stop=True,
             )
-            a_sb = pool.tile([P, j1 - j0], F32, name=f"a_sb{t}_{j0}")
+            accs.append(acc)
+        for (t, j0, j1), acc in zip(pieces, accs):
+            a_sb = pool.tile([P, j1 - j0], F32, name=f"a_sb{t}_{j0}", tag=f"a_sb{t % 2}_{j0}")
             nc.scalar.copy(out=a_sb[:], in_=acc[:])
-            staged.append(a_sb)
-        for (t, j0, j1), a_sb in zip(pieces, staged):
             nc.vector.tensor_copy(out=pw[t][:].indirect(l3[:, j0 // 16 : j1 // 16]), in_=a_sb[:])
 
         own, shared = [], []
@@ -150,20 +142,26 @@ def tile_picked_largercode_plain_one_ladder_store_plain_kernel(
             shared.append(pool.tile([P, S], F32, name=f"shared{t}"))
             nc.scalar.activation(out=own[t][:], in_=pw[t][:].indirect(l4[:]), func=COPY, scale=sa_sb[:, t : t + 1])
             nc.scalar.activation(out=shared[t][:], in_=pw[t][:].indirect(l5[:]), func=COPY, scale=sb_sb[:, t : t + 1])
-        pg = [pool.tile([P, S], F32, name=f"pg{t}") for t in range(PACK)]
+        pg = []
         for t in range(PACK):
+            if t == 0:
+                pg.append(pool.tile([P, S], F32, name="pg0", tag="a_sb1_0"))
+            else:
+                pg.append(pool.tile([P, S], F32, name=f"pg{t}", tag=f"own{t - 1}", align_bytes=64))
             nc.vector.tensor_tensor(out=pg[t][:], in0=own[t][:], in1=shared[t][:], op=MAX)
-        hid = pool.tile([P, PACK, O], BF16, name="hid")
+        hid = [pool.tile([P, 2, O], BF16, name=f"hid{i}") for i in range(2)]
         for t in range(PACK):
-            nc.scalar.activation(out=hid[:, t, :], in_=pg[t][:].indirect(l6[:]), func=COPY, scale=sd_sb[:, t : t + 1])
+            nc.scalar.activation(out=hid[t // 2][:, t % 2, :], in_=pg[t][:].indirect(l6[:]), func=COPY, scale=sd_sb[:, t : t + 1])
 
-        vs_sc = pool.tile([P, N], U8, name="vs_sc", tag="own2", align_bytes=64)
+        vs_sc = pool.tile([P, N], U8, name="vs_sc", tag="own3", align_bytes=64)
         nc.vector.tensor_copy(out=vs_sc[:], in_=vs_plane[:].indirect(l7[:]))
-        vs_codes = pool.tile([P, N], U32, name="vs_codes", tag="own3", align_bytes=64)
-        nc.vector.tensor_copy(out=vs_codes[:], in_=vs_raw[:].bitcast(U32).indirect(l7[:]))
 
         hid_il = pool.tile([P, PACK * O], BF16, name="hid_il", align_bytes=64)
-        interleave(nc, hid_il[:], hid[:])
+        for t in (0, 2):
+            nc.vector.tensor_copy(
+                out=hid_il[:].rearrange("p (c t) -> p c t", t=PACK)[:, :, t : t + 2],
+                in_=hid[t // 2][:].rearrange("p t c -> p c t"),
+            )
         h_codes = pool.tile([P, O], U32, name="h_codes", align_bytes=64)
         h_sc = pool.tile([P, O], U8, name="h_sc", align_bytes=64)
         nc.vector.quantize_mx(out=h_codes[:].bitcast(FP8X4), scales=h_sc[:], in_=hid_il[:])

@@ -71,14 +71,14 @@ def tile_picked_largercode_plain_one_ladder_store_plain_kernel(
         tb_sb[2] = load_rows(tb, 2, "tb2")
         ta_sb[3] = load_rows(ta, 3, "ta3")
         tb_sb[3] = load_rows(tb, 3, "tb3")
-        l3 = load_list(offs3, "l3")
-        l4 = load_list(offs4, "l4")
-        sa_sb = load_factor(sa, "sa_sb")
-        l5 = load_list(offs5, "l5")
-        sb_sb = load_factor(sb, "sb_sb")
         l7 = load_list(offs7, "l7")
         vs_raw = pool.tile([P, Z], I32, name="vs_raw")
         nc.sync.dma_start(vs_raw[:], vs_words[0].rearrange("p n t -> p (n t)").bitcast(I32))
+        l5 = load_list(offs5, "l5")
+        sb_sb = load_factor(sb, "sb_sb")
+        l4 = load_list(offs4, "l4")
+        sa_sb = load_factor(sa, "sa_sb")
+        l3 = load_list(offs3, "l3")
         l6 = load_list(offs6, "l6")
         sd_sb = load_factor(sd, "sd_sb")
         for q in range(4):

@@ -62,8 +62,6 @@ def tile_picked_largercode_plain_one_ladder_store_plain_kernel(
         l2 = load_list(offs2, "l2")
         gb_sb = load_factor(gb, "gb_sb")
         ta_sb[1] = load_rows(ta, 1, "ta1")
-        w_raw = pool.tile([P, 2 * R], U8, name="w_raw", align_bytes=64)
-        nc.sync.dma_start(w_raw[:].bitcast(I32), w_words[0].bitcast(I32))
         tb_sb[1] = load_rows(tb, 1, "tb1")
         w_stage = pool.tile([4, 4, R // 4], I32, name="w_stage")
         nc.sync.dma_start(w_stage[:], w_scales[0].bitcast(I32).rearrange("(q i) n -> i q n", i=4))
@@ -71,6 +69,8 @@ def tile_picked_largercode_plain_one_ladder_store_plain_kernel(
         tb_sb[2] = load_rows(tb, 2, "tb2")
         ta_sb[3] = load_rows(ta, 3, "ta3")
         tb_sb[3] = load_rows(tb, 3, "tb3")
+        w_raw = pool.tile([P, R], U16, name="w_raw")
+        nc.sync.dma_start(w_raw[:].bitcast(I32), w_words[0].bitcast(I32))
         l7 = load_list(offs7, "l7")
         vs_raw = pool.tile([P, Z], I32, name="vs_raw")
         nc.sync.dma_start(vs_raw[:], vs_words[0].rearrange("p n t -> p (n t)").bitcast(I32))
@@ -87,11 +87,6 @@ def tile_picked_largercode_plain_one_ladder_store_plain_kernel(
                 vs_scales[0, 4 * q : 4 * q + 4, :].bitcast(I32),
             )
 
-        w_codes = pool.tile([P, 2 * R], U8, name="w_codes", align_bytes=64)
-        nc.vector.tensor_copy(
-            out=w_codes[:].rearrange("p (t m b) -> p t m b", t=PACK, b=2),
-            in_=w_raw[:].rearrange("p (m t b) -> p t m b", t=PACK, b=2),
-        )
         for q in range(4):
             nc.vector.tensor_copy(out=w_plane[32 * q : 32 * q + 4, :].bitcast(I32), in_=w_stage[:, q, :])
         w_sc = pool.tile([P, R], U8, name="w_sc", align_bytes=64)
@@ -109,6 +104,11 @@ def tile_picked_largercode_plain_one_ladder_store_plain_kernel(
             for h in range(2):
                 cols = slice(h * HALF, (h + 1) * HALF)
                 nc.vector.tensor_tensor(out=xc_il[h][:, :, t], in0=pa[:, cols], in1=pb[:, cols], op=MAX)
+        w_codes = pool.tile([P, 2 * R], U8, name="w_codes", align_bytes=64)
+        nc.scalar.copy(
+            out=w_codes[:].bitcast(U16).rearrange("p (t m) -> p t m", t=PACK),
+            in_=w_raw[:].rearrange("p (m t) -> p t m", t=PACK),
+        )
         x_codes = pool.tile([P, J], U32, name="x_codes", align_bytes=64)
         x_sc = pool.tile([P, J], U8, name="x_sc", align_bytes=64)
         for h in range(2):

from contextlib import ExitStack

import concourse.mybir as mybir

K, J, R, T, U, C, O, S, N, Z = 512, 256, 512, 1024, 1024, 512, 128, 256, 256, 1024
FLOPS = 2 * K * R * J + 2 * R * N * O

F32 = mybir.dt.float32
BF16 = mybir.dt.bfloat16
I32 = mybir.dt.int32
U32 = mybir.dt.uint32
U16 = mybir.dt.uint16
U8 = mybir.dt.uint8
FP8X4 = mybir.dt.float8_e4m3fn_x4
FP4X4 = mybir.dt.float4_e2m1fn_x4
COPY = mybir.ActivationFunctionType.Copy
MAX = mybir.AluOpType.max

P = 128
PACK = 4
HALF = J // 2


def tile_picked_largercode_plain_one_ladder_store_plain_kernel(
    tc, ta, tb, ga, gb, w_words, w_scales, sa, sb, sd, vs_words, vs_scales,
    offs, offs2, offs3, offs4, offs5, offs6, offs7, out,
):
    nc = tc.nc
    with ExitStack() as ctx:
        lists = ctx.enter_context(tc.tile_pool(name="lists", bufs=1))
        pool = ctx.enter_context(tc.tile_pool(name="pool", bufs=1))
        psum = ctx.enter_context(tc.psum_pool(name="psum", bufs=1))

        def load_list(src, name):
            tile = lists.tile(list(src.shape), U16, name=name)
            nc.sync.dma_start(tile[:], src)
            return tile

        def load_factor(src, name):
            tile = pool.tile([P, PACK], F32, name=name, tag=name)
            nc.sync.dma_start(tile[:], src.rearrange("(p t) o -> p (t o)", t=PACK))
            return tile

        def load_rows(src, t, name):
            tile = pool.tile([P, src.shape[1]], F32, name=name)
            nc.sync.dma_start(tile[:], src.rearrange("(p t) c -> t p c", t=PACK)[t])
            return tile

        w_plane = pool.tile([P, R], U8, name="w_plane", align_bytes=64)
        nc.vector.memset(w_plane[:].bitcast(I32), 0)
        vs_plane = pool.tile([P, Z], U8, name="vs_plane", align_bytes=64)
        nc.vector.memset(vs_plane[:].bitcast(I32), 0)
        pw = [pool.tile([P, C], F32, name=f"pw{t}") for t in range(PACK)]
        for t in range(PACK):
            nc.vector.memset(pw[t][:], 0.0)

        ta_sb, tb_sb = {}, {}
        ta_sb[0] = load_rows(ta, 0, "ta0")
        l1 = load_list(offs, "l1")
        ga_sb = load_factor(ga, "ga_sb")
        tb_sb[0] = load_rows(tb, 0, "tb0")
        l2 = load_list(offs2, "l2")
        gb_sb = load_factor(gb, "gb_sb")
        ta_sb[1] = load_rows(ta, 1, "ta1")
        tb_sb[1] = load_rows(tb, 1, "tb1")
        w_stage = pool.tile([4, 4, R // 4], I32, name="w_stage")
        nc.sync.dma_start(w_stage[:], w_scales[0].bitcast(I32).rearrange("(q i) n -> i q n", i=4))
        ta_sb[2] = load_rows(ta, 2, "ta2")
        tb_sb[2] = load_rows(tb, 2, "tb2")
        ta_sb[3] = load_rows(ta, 3, "ta3")
        tb_sb[3] = load_rows(tb, 3, "tb3")
        w_raw = pool.tile([P, R], U16, name="w_raw")
        nc.sync.dma_start(w_raw[:].bitcast(I32), w_words[0].bitcast(I32))
        l7 = load_list(offs7, "l7")
        vs_raw = pool.tile([P, Z], I32, name="vs_raw")
        nc.sync.dma_start(vs_raw[:], vs_words[0].rearrange("p n t -> p (n t)").bitcast(I32))
        l5 = load_list(offs5, "l5")
        sb_sb = load_factor(sb, "sb_sb")
        l4 = load_list(offs4, "l4")
        sa_sb = load_factor(sa, "sa_sb")
        l3 = load_list(offs3, "l3")
        l6 = load_list(offs6, "l6")
        sd_sb = load_factor(sd, "sd_sb")
        for q in range(4):
            nc.sync.dma_start(
                vs_plane[32 * q : 32 * q + 4, :].bitcast(I32),
                vs_scales[0, 4 * q : 4 * q + 4, :].bitcast(I32),
            )

        for q in range(4):
            nc.vector.tensor_copy(out=w_plane[32 * q : 32 * q + 4, :].bitcast(I32), in_=w_stage[:, q, :])
        w_sc = pool.tile([P, R], U8, name="w_sc", align_bytes=64)
        nc.vector.tensor_copy(
            out=w_sc[:].rearrange("p (t m) -> p t m", t=PACK),
            in_=w_plane[:].rearrange("p (m t) -> p t m", t=PACK),
        )

        xc_il = [pool.tile([P, HALF, PACK], BF16, name=f"xc_il{h}", tag=f"xc_il{h}", align_bytes=64) for h in range(2)]
        for t in range(PACK):
            pa = pool.tile([P, J], F32, name=f"pa{t}")
            pb = pool.tile([P, J], F32, name=f"pb{t}")
            nc.scalar.activation(out=pa[:], in_=ta_sb[t][:].indirect(l1[:]), func=COPY, scale=ga_sb[:, t : t + 1])
            nc.scalar.activation(out=pb[:], in_=tb_sb[t][:].indirect(l2[:]), func=COPY, scale=gb_sb[:, t : t + 1])
            for h in range(2):
                cols = slice(h * HALF, (h + 1) * HALF)
                nc.vector.tensor_tensor(out=xc_il[h][:, :, t], in0=pa[:, cols], in1=pb[:, cols], op=MAX)
        w_codes = pool.tile([P, 2 * R], U8, name="w_codes", align_bytes=64)
        nc.scalar.copy(
            out=w_codes[:].bitcast(U16).rearrange("p (t m) -> p t m", t=PACK),
            in_=w_raw[:].rearrange("p (m t) -> p t m", t=PACK),
        )
        x_codes = pool.tile([P, J], U32, name="x_codes", align_bytes=64)
        x_sc = pool.tile([P, J], U8, name="x_sc", align_bytes=64)
        for h in range(2):
            cols = slice(h * HALF, (h + 1) * HALF)
            nc.vector.quantize_mx(out=x_codes[:, cols].bitcast(FP8X4), scales=x_sc[:, cols], in_=xc_il[h][:].rearrange("p c t -> p (c t)"))

        vs_codes = pool.tile([P, N], U32, name="vs_codes", tag="xc_il1", align_bytes=64)
        nc.vector.tensor_copy(out=vs_codes[:], in_=vs_raw[:].bitcast(U32).indirect(l7[:]))
        pieces = [(0, 0, HALF), (1, 0, HALF), (0, HALF, J), (1, HALF, J), (2, 0, J), (3, 0, J)]
        accs = []
        for t, j0, j1 in pieces:
            acc = psum.tile([P, j1 - j0], F32, name=f"a_ps{t}_{j0}")
            nc.tensor.matmul_mx(
                out=acc[:],
                lhsT=w_codes[:, 2 * P * t : 2 * P * (t + 1)].bitcast(FP4X4),
                lhsT_scale=w_sc[:, P * t : P * (t + 1)],
                rhs=x_codes[:, j0:j1].bitcast(FP8X4),
                rhs_scale=x_sc[:, j0:j1],
                start=True,
                stop=True,
            )
            accs.append(acc)
        for (t, j0, j1), acc in zip(pieces, accs):
            a_sb = pool.tile([P, j1 - j0], F32, name=f"a_sb{t}_{j0}", tag=f"a_sb{t % 2}_{j0}")
            nc.scalar.copy(out=a_sb[:], in_=acc[:])
            nc.vector.tensor_copy(out=pw[t][:].indirect(l3[:, j0 // 16 : j1 // 16]), in_=a_sb[:])

        own, shared = [], []
        for t in range(PACK):
            own.append(pool.tile([P, S], F32, name=f"own{t}", tag=f"own{t}", align_bytes=64))
            shared.append(pool.tile([P, S], F32, name=f"shared{t}"))
            nc.scalar.activation(out=own[t][:], in_=pw[t][:].indirect(l4[:]), func=COPY, scale=sa_sb[:, t : t + 1])
            nc.scalar.activation(out=shared[t][:], in_=pw[t][:].indirect(l5[:]), func=COPY, scale=sb_sb[:, t : t + 1])
        pg = []
        for t in range(PACK):
            if t == 0:
                pg.append(pool.tile([P, S], F32, name="pg0", tag="a_sb1_0"))
            else:
                pg.append(pool.tile([P, S], F32, name=f"pg{t}", tag=f"own{t - 1}", align_bytes=64))
            nc.vector.tensor_tensor(out=pg[t][:], in0=own[t][:], in1=shared[t][:], op=MAX)
        hid = [pool.tile([P, 2, O], BF16, name=f"hid{i}") for i in range(2)]
        for t in range(PACK):
            nc.scalar.activation(out=hid[t // 2][:, t % 2, :], in_=pg[t][:].indirect(l6[:]), func=COPY, scale=sd_sb[:, t : t + 1])

        vs_sc = pool.tile([P, N], U8, name="vs_sc", tag="own3", align_bytes=64)
        nc.vector.tensor_copy(out=vs_sc[:], in_=vs_plane[:].indirect(l7[:]))

        hid_il = pool.tile([P, PACK * O], BF16, name="hid_il", align_bytes=64)
        for t in (0, 2):
            nc.vector.tensor_copy(
                out=hid_il[:].rearrange("p (c t) -> p c t", t=PACK)[:, :, t : t + 2],
                in_=hid[t // 2][:].rearrange("p t c -> p c t"),
            )
        h_codes = pool.tile([P, O], U32, name="h_codes", align_bytes=64)
        h_sc = pool.tile([P, O], U8, name="h_sc", align_bytes=64)
        nc.vector.quantize_mx(out=h_codes[:].bitcast(FP8X4), scales=h_sc[:], in_=hid_il[:])
        for u in range(2):
            rows = slice(u * P, (u + 1) * P)
            y_ps = psum.tile([P, O], F32, name=f"y_ps{u}")
            nc.tensor.matmul_mx(
                out=y_ps[:],
                lhsT=vs_codes[:, rows].bitcast(FP8X4),
                lhsT_scale=vs_sc[:, rows],
                rhs=h_codes[:].bitcast(FP8X4),
                rhs_scale=h_sc[:],
                start=True,
                stop=True,
            )
            y_sb = pool.tile([P, O], F32, name=f"y_sb{u}")
            if u == 0:
                nc.scalar.copy(out=y_sb[:], in_=y_ps[:])
                nc.scalar.dma_start(out[rows, :], y_sb[:])
            else:
                nc.vector.tensor_copy(out=y_sb[:], in_=y_ps[:])
                nc.sync.dma_start(out[rows, :], y_sb[:])
